import numpy as np
import ml_dtypes


def mxq(x, axis, fmt="e4m3"):
    dtype, down = {"e4m3": (ml_dtypes.float8_e4m3fn, 7), "e5m2": (ml_dtypes.float8_e5m2, 14)}[fmt]
    v = np.moveaxis(np.asarray(x, np.float32).astype(ml_dtypes.bfloat16).astype(np.float64), axis, -1)
    blocks = v.reshape(v.shape[:-1] + (-1, 32))
    amax = np.abs(blocks).max(-1, keepdims=True)
    byte = np.maximum(np.where(amax > 0, np.frexp(amax)[1] - 1 + 127, 0) - down, 1)
    scale = np.exp2(byte - 127.0)
    codes = (blocks / scale).astype(np.float32).astype(dtype).astype(np.float64)
    return np.moveaxis((codes * scale).reshape(v.shape), -1, axis)


WIDE = False


def mx_kscale(k):
    if not WIDE:
        return np.ones(k)
    levels = np.array([10, -10, 5, -5, 0])
    if k % 512:
        return np.exp2(np.random.permutation(np.resize(levels, k // 32))).repeat(32)
    a = np.empty((k // 512, 16))
    for p in range(k // 512):
        a[p, :8] = np.random.permutation(np.resize(levels, 8))
        for g in range(8):
            far = levels[np.abs(levels - a[p, g]) >= 10]
            a[p, g + 8] = far[np.random.randint(len(far))]
    return np.exp2(a.ravel()).repeat(32)


def f64(x):
    return np.asarray(x).astype(np.float64)


def striped(idx):
    return np.tile(np.asarray(idx).reshape(-1, 16).T, (8, 1)).astype(np.uint16)


def unstriped(offs):
    return offs[:16].T.reshape(-1).astype(np.int64)


E2M1 = np.array([0.0, 0.5, 1.0, 1.5, 2.0, 3.0, 4.0, 6.0, -0.0, -0.5, -1.0, -1.5, -2.0, -3.0, -4.0, -6.0])


def pack_weight(w, fmt):
    k, n = w.shape
    w = f64(np.asarray(w, np.float32).astype(ml_dtypes.bfloat16)).reshape(k // 32, 32, n)
    amax = np.abs(w).max(1)
    if fmt == "e4m3":
        byte = np.frexp(amax)[1] - 1 + 127 - 7
    else:
        mant, ex = np.frexp(amax / 6.0)
        byte = np.where(mant > 0.5, ex, ex - 1) + 127
    byte = np.clip(np.where(amax > 0, byte, 1), 1, 254)
    scaled = (w * np.exp2(127.0 - byte)[:, None, :]).reshape(k, n).astype(np.float32)
    by_word = np.ascontiguousarray(scaled.reshape(k // 512, 128, 4, n).transpose(0, 1, 3, 2))
    if fmt == "e4m3":
        words = by_word.astype(ml_dtypes.float8_e4m3fn).view(np.uint8)
    else:
        c = by_word.astype(ml_dtypes.float4_e2m1fn).view(np.uint8) & 0xF
        words = (c[..., 0::2] | (c[..., 1::2] << 4)).reshape(k // 512, 128, 2 * n)
    return np.ascontiguousarray(words), np.ascontiguousarray(byte.astype(np.uint8).reshape(k // 512, 16, n))


def unpack_weight(words, scales, fmt):
    g, _, n = scales.shape
    words = np.ascontiguousarray(words).reshape(g, 128, n, -1)
    if fmt == "e4m3":
        vals = words.view(ml_dtypes.float8_e4m3fn).astype(np.float64)
    else:
        nib = np.empty((g, 128, n, 4), np.uint8)
        nib[..., 0::2] = words & 0xF
        nib[..., 1::2] = words >> 4
        vals = E2M1[nib]
    vals = vals * np.repeat(np.exp2(scales.astype(np.float64) - 127.0), 8, axis=1)[..., None]
    return vals.transpose(0, 1, 3, 2).reshape(g * 512, n)


def sigmoid(v):
    return 1.0 / (1.0 + np.exp(-v))


D, T, I, Q, E, U, M = 512, 2048, 512, 256, 512, 1024, 1024


def setup_inputs():
    n = np.random.standard_normal
    idx = np.random.permutation(T)[:I]
    idx2 = np.random.permutation(U)[:I]
    idx3 = np.random.permutation(M)[:Q]
    fd = mx_kscale(D)
    fi = mx_kscale(I)
    ti = np.ones(T)
    ti[idx] = fi
    keysp = pack_weight(n((D, T)) / fd[:, None], "e4m3")
    return {
        "query": (n((D, Q)) * 0.7 / np.sqrt(D) * fd[:, None]).astype(np.float32),
        "query2": (n((D, Q)) * 0.7 / np.sqrt(D) * fd[:, None]).astype(np.float32),
        "keys_words": keysp[0],
        "keys_scales": keysp[1],
        "notes": (n((D, U)) / fd[:, None]).astype(np.float32),
        "os": (np.random.uniform(0.02, 0.08, (1, I)) * fi).astype(np.float32),
        "vals": (n((E, T)) / ti).astype(np.float32),
        "old": (n((E, M)) * 0.7).astype(np.float32),
        "offs": striped(idx),
        "offs2": striped(idx2),
        "offs3": striped(idx3),
    }


def reference(query, query2, keys_words, keys_scales, notes, os, vals, old, offs, offs2, offs3):
    idx = unstriped(offs)
    idx2 = unstriped(offs2)
    idx3 = unstriped(offs3)
    keysu = unpack_weight(keys_words, keys_scales, "e4m3")
    queryq = mxq(f64(query), 0, "e4m3")
    keysidxg = keysu[:, idx]
    query2q = mxq(f64(query2), 0, "e4m3")
    notesidx2q = mxq(f64(notes)[:, idx2], 0, "e4m3")
    s = queryq.T @ keysidxg + query2q.T @ notesidx2q
    w = sigmoid(s)
    wo1 = w * f64(os)
    wt1 = wo1.T
    vt1 = f64(vals)[:, idx].T
    vt1q = mxq(vt1, 0, "e4m3")
    wt1q = mxq(wt1, 0, "e4m3")
    o = vt1q.T @ wt1q
    of = np.zeros((E, M))
    of[:, idx3] = o
    y = np.maximum(of, f64(old)) + f64(old) * 0.25
    return y

@@ -1,0 +1,243 @@
+from contextlib import ExitStack
+
+import concourse.mybir as mybir
+from concourse.masks import make_identity
+
+D, T, I, Q, E, U, M = 512, 2048, 512, 256, 512, 1024, 1024
+FLOPS = 2 * (2 * D * Q * I) + 2 * I * E * Q
+
+F32 = mybir.dt.float32
+BF16 = mybir.dt.bfloat16
+I32 = mybir.dt.int32
+U32 = mybir.dt.uint32
+U16 = mybir.dt.uint16
+U8 = mybir.dt.uint8
+FP8X4 = mybir.dt.float8_e4m3fn_x4
+ACT = mybir.ActivationFunctionType
+ALU = mybir.AluOpType
+
+P = 128
+PACK = 4
+Q_BLOCKS = Q // P
+E_BLOCKS = E // P
+HALF = M // 2
+
+
+def tile_attend_twosources_keptlarger_lean_kernel(
+    tc, query, query2, keys_words, keys_scales, notes, slot_factor, vals, old, offs, offs2, offs3, out
+):
+    nc = tc.nc
+
+    with ExitStack() as ctx:
+        sb = ctx.enter_context(tc.tile_pool(name="sb", bufs=1))
+        ps_one = ctx.enter_context(tc.psum_pool(name="ps_one", bufs=1))
+        ps_two = ctx.enter_context(tc.psum_pool(name="ps_two", bufs=2))
+
+        def tile(shape, dtype, name, tag=""):
+            return sb.tile(shape, dtype, name=name, tag=tag or name, align_bytes=64)
+
+        def quantize(values, width, name, tag=""):
+            codes = tile([P, width], U32, name + "_codes", tag)
+            scales = tile([P, width], U8, name + "_scales")
+            nc.vector.quantize_mx(out=codes[:].bitcast(FP8X4), scales=scales[:], in_=values)
+            return codes, scales
+
+        tok_list = tile([P, I // 16], U16, "tok_list")
+        note_list = tile([P, I // 16], U16, "note_list")
+        col_list = tile([P, Q // 16], U16, "col_list")
+        note_planes = [tile([P, U], F32, "note_plane%d" % j) for j in range(PACK)]
+        q_raw = tile([P, PACK, Q], F32, "q_raw")
+        q2_raw = tile([P, PACK, Q], F32, "q2_raw")
+        key_pool = tile([P, T], I32, "key_pool")
+        scale_pool = tile([P, T], U8, "scale_pool")
+        factor = tile([P, PACK], F32, "factor")
+        val_pool = [tile([P, T], F32, "val_pool%d" % b) for b in range(E_BLOCKS)]
+        old_rows = [tile([P, M], F32, "old_rows%d" % b) for b in range(E_BLOCKS)]
+        placed = [tile([P, M], F32, "placed%d" % b) for b in range(E_BLOCKS)]
+
+        nc.gpsimd.memset(scale_pool[:].bitcast(I32), 0)
+        scale_rows = keys_scales[0].bitcast(I32)
+        notes_by_plane = notes.rearrange("(p j) u -> j p u", j=PACK)
+        nc.sync.dma_start(out=note_list[:], in_=offs2)
+        nc.sync.dma_start(out=note_planes[0][:], in_=notes_by_plane[0])
+        nc.sync.dma_start(out=tok_list[:], in_=offs)
+        for quad in range(4):
+            nc.sync.dma_start(
+                out=scale_pool[32 * quad : 32 * quad + 4, :].bitcast(I32), in_=scale_rows[4 * quad : 4 * quad + 4, :]
+            )
+        for j in range(1, PACK):
+            nc.sync.dma_start(out=note_planes[j][:], in_=notes_by_plane[j])
+        nc.sync.dma_start(out=q2_raw[:], in_=query2.rearrange("(p j) q -> p j q", j=PACK))
+        nc.sync.dma_start(out=q_raw[:], in_=query.rearrange("(p j) q -> p j q", j=PACK))
+        nc.sync.dma_start(out=key_pool[:], in_=keys_words[0].rearrange("p t r -> p (t r)").bitcast(I32))
+        nc.sync.dma_start(out=factor[:], in_=slot_factor.rearrange("o (p r) -> (o p) r", r=PACK))
+        nc.sync.dma_start(out=col_list[:], in_=offs3)
+
+        def load_vals(b):
+            nc.sync.dma_start(out=val_pool[b][:], in_=vals[b * P : (b + 1) * P, :])
+
+        def load_old(b):
+            nc.sync.dma_start(out=old_rows[b][:], in_=old[b * P : (b + 1) * P, :])
+
+        for b in range(E_BLOCKS):
+            load_vals(b)
+        for b in range(E_BLOCKS):
+            load_old(b)
+
+        ident = tile([P, P], F32, "ident")
+        make_identity(nc, ident[:])
+        for b in range(E_BLOCKS):
+            nc.gpsimd.memset(placed[b][:], 0.0)
+
+        key_scales = tile([P, I], U8, "key_scales")
+        nc.vector.tensor_copy(out=key_scales[:], in_=scale_pool[:].indirect(tok_list[:]))
+
+        note_picked = tile([P, PACK, I], BF16, "note_picked")
+        for j in range(PACK):
+            window = note_planes[j][:].indirect(note_list[:])
+            if j % 2 == 0:
+                nc.scalar.activation(out=note_picked[:, j, :], in_=window, func=ACT.Copy)
+            else:
+                nc.vector.tensor_copy(out=note_picked[:, j, :], in_=window)
+        note_grouped = tile([P, I, PACK], BF16, "note_grouped")
+        nc.vector.tensor_copy(
+            out=note_grouped[:], in_=note_picked[:].rearrange("p j i -> p i j")
+        )
+        q2_grouped = tile([P, Q, PACK], BF16, "q2_grouped")
+        q_grouped = tile([P, Q, PACK], BF16, "q_grouped")
+        for grouped, raw in ((q2_grouped, q2_raw), (q_grouped, q_raw)):
+            nc.scalar.copy(
+                out=grouped[:], in_=raw[:].rearrange("p j q -> p q j")
+            )
+        note_codes, note_scales = quantize(note_grouped[:].rearrange("p i j -> p (i j)"), I, "note")
+        q2_codes, q2_scales = quantize(q2_grouped[:].rearrange("p q j -> p (q j)"), Q, "q2")
+        q_codes, q_scales = quantize(q_grouped[:].rearrange("p q j -> p (q j)"), Q, "q")
+        key_codes = tile([P, I], U32, "key_codes")
+        nc.vector.tensor_copy(out=key_codes[:], in_=key_pool[:].bitcast(U32).indirect(tok_list[:]))
+
+        scores = [ps_one.tile([P, I], F32, name="scores%d" % h) for h in range(Q_BLOCKS)]
+        for lhs_codes, lhs_scales, rhs_codes, rhs_scales, first in (
+            (q2_codes, q2_scales, note_codes, note_scales, True),
+            (q_codes, q_scales, key_codes, key_scales, False),
+        ):
+            for h in range(Q_BLOCKS):
+                cols = slice(h * P, (h + 1) * P)
+                nc.tensor.matmul_mx(
+                    out=scores[h][:],
+                    lhsT=lhs_codes[:, cols].bitcast(FP8X4),
+                    lhsT_scale=lhs_scales[:, cols],
+                    rhs=rhs_codes[:].bitcast(FP8X4),
+                    rhs_scale=rhs_scales[:],
+                    start=first,
+                    stop=not first,
+                )
+
+        def pick_vals(b, on_vector, tag):
+            picked = tile([P, I], BF16, "val_picked%d" % b, tag)
+            window = val_pool[b][:].indirect(tok_list[:])
+            if on_vector:
+                nc.vector.tensor_copy(out=picked[:], in_=window)
+            else:
+                nc.scalar.activation(out=picked[:], in_=window, func=ACT.Copy)
+            return picked
+
+        def turn_vals(picked, pair_words):
+            pairs = picked[:].bitcast(F32)
+            turned = ps_two.tile([P, 2, P], F32, name="val_turned")
+            for u in range(2):
+                nc.tensor.transpose(turned[:, u, :], pairs[:, u::2], ident[:])
+            nc.scalar.copy(out=pair_words.rearrange("p (e u) -> p e u", u=2), in_=turned[:].rearrange("p u e -> p e u"))
+
+        def quantize_vals(b, pair_words, tag):
+            return quantize(pair_words.bitcast(BF16), P, "val%d" % b, tag)
+
+        sigs = []
+        for h in range(Q_BLOCKS):
+            sig = tile([P, PACK, P], F32, "sig%d" % h)
+            nc.scalar.activation(out=sig[:], in_=scores[h][:].rearrange("q (s r) -> q r s", r=PACK), func=ACT.Sigmoid)
+            sigs.append(sig)
+        picked0 = pick_vals(0, True, "q_grouped")
+        w_grouped = tile([P, Q, PACK], BF16, "w_grouped", "val_pool0")
+        for h in range(Q_BLOCKS):
+            sig_turned = ps_one.tile([P, PACK, P], F32, name="sig_turned%d" % h)
+            for r in range(PACK):
+                nc.tensor.transpose(sig_turned[:, r, :], sigs[h][:, r, :], ident[:])
+            nc.vector.tensor_tensor(
+                out=w_grouped[:, h * P : (h + 1) * P, :],
+                in0=sig_turned[:].rearrange("s r q -> s q r"),
+                in1=factor[:].unsqueeze(1).to_broadcast([P, P, PACK]),
+                op=ALU.mult,
+            )
+        words0 = tile([P, 2 * P], F32, "words0")
+        turn_vals(picked0, words0[:])
+        val0 = quantize_vals(0, words0[:], "")
+        w_codes, w_scales = quantize(w_grouped[:].rearrange("s q r -> s (q r)"), Q, "w")
+
+        def multiply(val_mx):
+            val_codes, val_scales = val_mx
+            acc = ps_two.tile([P, Q], F32, name="acc")
+            nc.tensor.matmul_mx(
+                out=acc[:],
+                lhsT=val_codes[:].bitcast(FP8X4),
+                lhsT_scale=val_scales[:],
+                rhs=w_codes[:].bitcast(FP8X4),
+                rhs_scale=w_scales[:],
+                start=True,
+                stop=True,
+            )
+            return acc
+
+        def place_on_vector(b, h, acc, tag):
+            dense = tile([P, P], F32, "dense%d_%d" % (b, h), tag)
+            nc.vector.tensor_copy(out=dense[:], in_=acc[:, h * P : (h + 1) * P])
+            listed = col_list[:, h * (P // 16) : (h + 1) * (P // 16)]
+            nc.vector.tensor_copy(out=placed[b][:].indirect(listed), in_=dense[:])
+
+        def place_on_scalar(b, dense):
+            nc.scalar.activation(out=placed[b][:].indirect(col_list[:]), in_=dense, func=ACT.Copy)
+
+        def merge_larger(b, tag):
+            larger = [tile([P, HALF], F32, "larger%d_%d" % (b, k), tag if k == 0 else "") for k in range(2)]
+            for k in range(2):
+                cols = slice(k * HALF, (k + 1) * HALF)
+                nc.vector.tensor_tensor(out=larger[k][:], in0=placed[b][:, cols], in1=old_rows[b][:, cols], op=ALU.max)
+            return larger
+
+        def merge_store(b, k, larger, tag):
+            cols = slice(k * HALF, (k + 1) * HALF)
+            result = tile([P, HALF], F32, "result%d_%d" % (b, k), tag)
+            nc.vector.scalar_tensor_tensor(
+                out=result[:], in0=old_rows[b][:, cols], scalar=0.25, in1=larger[k][:], op0=ALU.mult, op1=ALU.add
+            )
+            nc.sync.dma_start(out=out[b * P : (b + 1) * P, cols], in_=result[:])
+            return result
+
+        def merge(b, tag=""):
+            larger = merge_larger(b, tag)
+            return [merge_store(b, k, larger, "") for k in range(2)]
+
+        words1 = tile([P, 2 * P], F32, "words1")
+        turn_vals(pick_vals(1, False, "sig0"), words1[:])
+        picked2 = pick_vals(2, False, "sig0")
+        picked3 = pick_vals(3, False, "")
+        acc0 = multiply(val0)
+        place_on_vector(0, 0, acc0, "")
+        val_mx = quantize_vals(1, words1[:], "dense0_0")
+        place_on_vector(0, 1, acc0, "words1")
+        for b, picked in ((1, picked2), (2, picked3), (3, None)):
+            stage = tile([P, Q + 2 * P], F32, "stage%d" % b, "val_pool3")
+            dense, words = stage[:, :Q], stage[:, Q:]
+            if b == 2:
+                turn_vals(picked, words)
+            nc.scalar.copy(out=dense, in_=multiply(val_mx)[:])
+            if b == 1:
+                turn_vals(picked, words)
+            place_on_scalar(b, dense)
+            larger = merge_larger(b - 1, "")
+            if b == 2:
+                val_mx = quantize_vals(b + 1, words, "larger0_1")
+            merge_store(b - 1, 0, larger, "")
+            if b == 1:
+                val_mx = quantize_vals(b + 1, words, "placed0")
+            merge_store(b - 1, 1, larger, "")
+        merge(3)

@@ -87,7 +87,8 @@ def tile_attend_twosources_keptlarger_lean_kernel(
         ident = tile([P, P], F32, "ident")
         make_identity(nc, ident[:])
         for b in range(E_BLOCKS):
-            nc.gpsimd.memset(placed[b][:], 0.0)
+            engine = nc.gpsimd if b == E_BLOCKS - 1 else nc.vector
+            engine.memset(placed[b][:], 0.0)
 
         key_scales = tile([P, I], U8, "key_scales")
         nc.vector.tensor_copy(out=key_scales[:], in_=scale_pool[:].indirect(tok_list[:]))
@@ -168,10 +169,11 @@ def tile_attend_twosources_keptlarger_lean_kernel(
                 in1=factor[:].unsqueeze(1).to_broadcast([P, P, PACK]),
                 op=ALU.mult,
             )
-        words0 = tile([P, 2 * P], F32, "words0")
+        picked1 = pick_vals(1, False, "sig0")
+        words0 = tile([P, 2 * P], F32, "words0", "val_pool1")
         turn_vals(picked0, words0[:])
-        val0 = quantize_vals(0, words0[:], "")
         w_codes, w_scales = quantize(w_grouped[:].rearrange("s q r -> s (q r)"), Q, "w")
+        val0 = quantize_vals(0, words0[:], "")
 
         def multiply(val_mx):
             val_codes, val_scales = val_mx
@@ -187,20 +189,13 @@ def tile_attend_twosources_keptlarger_lean_kernel(
             )
             return acc
 
-        def place_on_vector(b, h, acc, tag):
-            dense = tile([P, P], F32, "dense%d_%d" % (b, h), tag)
-            nc.vector.tensor_copy(out=dense[:], in_=acc[:, h * P : (h + 1) * P])
-            listed = col_list[:, h * (P // 16) : (h + 1) * (P // 16)]
-            nc.vector.tensor_copy(out=placed[b][:].indirect(listed), in_=dense[:])
-
         def place_on_scalar(b, dense):
             nc.scalar.activation(out=placed[b][:].indirect(col_list[:]), in_=dense, func=ACT.Copy)
 
-        def merge_larger(b, tag):
-            larger = [tile([P, HALF], F32, "larger%d_%d" % (b, k), tag if k == 0 else "") for k in range(2)]
-            for k in range(2):
-                cols = slice(k * HALF, (k + 1) * HALF)
-                nc.vector.tensor_tensor(out=larger[k][:], in0=placed[b][:, cols], in1=old_rows[b][:, cols], op=ALU.max)
+        def merge_larger(b, k):
+            cols = slice(k * HALF, (k + 1) * HALF)
+            larger = tile([P, HALF], F32, "larger%d_%d" % (b, k))
+            nc.vector.tensor_tensor(out=larger[:], in0=placed[b][:, cols], in1=old_rows[b][:, cols], op=ALU.max)
             return larger
 
         def merge_store(b, k, larger, tag):
@@ -213,17 +208,18 @@ def tile_attend_twosources_keptlarger_lean_kernel(
             return result
 
         def merge(b, tag=""):
-            larger = merge_larger(b, tag)
+            larger = [merge_larger(b, k) for k in range(2)]
             return [merge_store(b, k, larger, "") for k in range(2)]
 
         words1 = tile([P, 2 * P], F32, "words1")
-        turn_vals(pick_vals(1, False, "sig0"), words1[:])
+        turn_vals(picked1, words1[:])
         picked2 = pick_vals(2, False, "sig0")
         picked3 = pick_vals(3, False, "")
         acc0 = multiply(val0)
-        place_on_vector(0, 0, acc0, "")
-        val_mx = quantize_vals(1, words1[:], "dense0_0")
-        place_on_vector(0, 1, acc0, "words1")
+        val_mx = quantize_vals(1, words1[:], "val_pool1")
+        dense0 = tile([P, Q], F32, "dense0", "words1")
+        nc.vector.tensor_copy(out=dense0[:], in_=acc0[:])
+        nc.vector.tensor_copy(out=placed[0][:].indirect(col_list[:]), in_=dense0[:])
         for b, picked in ((1, picked2), (2, picked3), (3, None)):
             stage = tile([P, Q + 2 * P], F32, "stage%d" % b, "val_pool3")
             dense, words = stage[:, :Q], stage[:, Q:]
@@ -233,9 +229,10 @@ def tile_attend_twosources_keptlarger_lean_kernel(
             if b == 1:
                 turn_vals(picked, words)
             place_on_scalar(b, dense)
-            larger = merge_larger(b - 1, "")
+            larger = [merge_larger(b - 1, 0)]
             if b == 2:
                 val_mx = quantize_vals(b + 1, words, "larger0_1")
+            larger.append(merge_larger(b - 1, 1))
             merge_store(b - 1, 0, larger, "")
             if b == 1:
                 val_mx = quantize_vals(b + 1, words, "placed0")

@@ -213,28 +213,26 @@ def tile_attend_twosources_keptlarger_lean_kernel(
 
         words1 = tile([P, 2 * P], F32, "words1")
         turn_vals(picked1, words1[:])
-        picked2 = pick_vals(2, False, "sig0")
-        picked3 = pick_vals(3, False, "")
-        acc0 = multiply(val0)
-        val_mx = quantize_vals(1, words1[:], "val_pool1")
-        dense0 = tile([P, Q], F32, "dense0", "words1")
-        nc.vector.tensor_copy(out=dense0[:], in_=acc0[:])
-        nc.vector.tensor_copy(out=placed[0][:].indirect(col_list[:]), in_=dense0[:])
+        picked2 = pick_vals(2, True, "val_pool1")
+        dense0 = tile([P, Q], F32, "dense0", "stage")
+        nc.scalar.copy(out=dense0[:], in_=multiply(val0)[:])
+        place_on_scalar(0, dense0[:])
+        val_mx = quantize_vals(1, words1[:], "val_pool2")
+        picked3 = pick_vals(3, True, "words1")
         for b, picked in ((1, picked2), (2, picked3), (3, None)):
-            stage = tile([P, Q + 2 * P], F32, "stage%d" % b, "val_pool3")
+            stage = tile([P, Q + 2 * P], F32, "stage%d" % b, "stage")
             dense, words = stage[:, :Q], stage[:, Q:]
             if b == 2:
                 turn_vals(picked, words)
             nc.scalar.copy(out=dense, in_=multiply(val_mx)[:])
             if b == 1:
                 turn_vals(picked, words)
+                val_mx = quantize_vals(b + 1, words, "val_pool3")
             place_on_scalar(b, dense)
             larger = [merge_larger(b - 1, 0)]
             if b == 2:
                 val_mx = quantize_vals(b + 1, words, "larger0_1")
             larger.append(merge_larger(b - 1, 1))
             merge_store(b - 1, 0, larger, "")
-            if b == 1:
-                val_mx = quantize_vals(b + 1, words, "placed0")
             merge_store(b - 1, 1, larger, "")
         merge(3)

@@ -58,15 +58,16 @@ def tile_attend_twosources_keptlarger_lean_kernel(
         nc.gpsimd.memset(scale_pool[:].bitcast(I32), 0)
         scale_rows = keys_scales[0].bitcast(I32)
         notes_by_plane = notes.rearrange("(p j) u -> j p u", j=PACK)
-        nc.sync.dma_start(out=note_list[:], in_=offs2)
         nc.sync.dma_start(out=note_planes[0][:], in_=notes_by_plane[0])
+        nc.sync.dma_start(out=note_list[:], in_=offs2)
+        nc.sync.dma_start(out=note_planes[1][:], in_=notes_by_plane[1])
         nc.sync.dma_start(out=tok_list[:], in_=offs)
+        nc.sync.dma_start(out=note_planes[2][:], in_=notes_by_plane[2])
         for quad in range(4):
             nc.sync.dma_start(
                 out=scale_pool[32 * quad : 32 * quad + 4, :].bitcast(I32), in_=scale_rows[4 * quad : 4 * quad + 4, :]
             )
-        for j in range(1, PACK):
-            nc.sync.dma_start(out=note_planes[j][:], in_=notes_by_plane[j])
+        nc.sync.dma_start(out=note_planes[3][:], in_=notes_by_plane[3])
         nc.sync.dma_start(out=q2_raw[:], in_=query2.rearrange("(p j) q -> p j q", j=PACK))
         nc.sync.dma_start(out=q_raw[:], in_=query.rearrange("(p j) q -> p j q", j=PACK))
         nc.sync.dma_start(out=key_pool[:], in_=keys_words[0].rearrange("p t r -> p (t r)").bitcast(I32))
@@ -214,19 +215,18 @@ def tile_attend_twosources_keptlarger_lean_kernel(
         words1 = tile([P, 2 * P], F32, "words1")
         turn_vals(picked1, words1[:])
         picked2 = pick_vals(2, True, "val_pool1")
-        dense0 = tile([P, Q], F32, "dense0", "stage")
+        dense0 = tile([P, Q], F32, "dense0")
         nc.scalar.copy(out=dense0[:], in_=multiply(val0)[:])
         place_on_scalar(0, dense0[:])
         val_mx = quantize_vals(1, words1[:], "val_pool2")
         picked3 = pick_vals(3, True, "words1")
         for b, picked in ((1, picked2), (2, picked3), (3, None)):
-            stage = tile([P, Q + 2 * P], F32, "stage%d" % b, "stage")
-            dense, words = stage[:, :Q], stage[:, Q:]
-            if b == 2:
-                turn_vals(picked, words)
+            dense = tile([P, Q], F32, "dense%d" % b)[:]
             nc.scalar.copy(out=dense, in_=multiply(val_mx)[:])
-            if b == 1:
+            if b < 3:
+                words = tile([P, 2 * P], F32, "words%d" % (b + 1))[:]
                 turn_vals(picked, words)
+            if b == 1:
                 val_mx = quantize_vals(b + 1, words, "val_pool3")
             place_on_scalar(b, dense)
             larger = [merge_larger(b - 1, 0)]

@@ -63,10 +63,8 @@ def tile_attend_twosources_keptlarger_lean_kernel(
         nc.sync.dma_start(out=note_planes[1][:], in_=notes_by_plane[1])
         nc.sync.dma_start(out=tok_list[:], in_=offs)
         nc.sync.dma_start(out=note_planes[2][:], in_=notes_by_plane[2])
-        for quad in range(4):
-            nc.sync.dma_start(
-                out=scale_pool[32 * quad : 32 * quad + 4, :].bitcast(I32), in_=scale_rows[4 * quad : 4 * quad + 4, :]
-            )
+        for r in range(4):
+            nc.sync.dma_start(out=scale_pool[r:P:32, :].bitcast(I32), in_=scale_rows[r:16:4, :])
         nc.sync.dma_start(out=note_planes[3][:], in_=notes_by_plane[3])
         nc.sync.dma_start(out=q2_raw[:], in_=query2.rearrange("(p j) q -> p j q", j=PACK))
         nc.sync.dma_start(out=q_raw[:], in_=query.rearrange("(p j) q -> p j q", j=PACK))

from contextlib import ExitStack

import concourse.mybir as mybir
from concourse.masks import make_identity

D, T, I, Q, E, U, M = 512, 2048, 512, 256, 512, 1024, 1024
FLOPS = 2 * (2 * D * Q * I) + 2 * I * E * Q

F32 = mybir.dt.float32
BF16 = mybir.dt.bfloat16
I32 = mybir.dt.int32
U32 = mybir.dt.uint32
U16 = mybir.dt.uint16
U8 = mybir.dt.uint8
FP8X4 = mybir.dt.float8_e4m3fn_x4
ACT = mybir.ActivationFunctionType
ALU = mybir.AluOpType

P = 128
PACK = 4
Q_BLOCKS = Q // P
E_BLOCKS = E // P
HALF = M // 2


def tile_attend_twosources_keptlarger_lean_kernel(
    tc, query, query2, keys_words, keys_scales, notes, slot_factor, vals, old, offs, offs2, offs3, out
):
    nc = tc.nc

    with ExitStack() as ctx:
        sb = ctx.enter_context(tc.tile_pool(name="sb", bufs=1))
        ps_one = ctx.enter_context(tc.psum_pool(name="ps_one", bufs=1))
        ps_two = ctx.enter_context(tc.psum_pool(name="ps_two", bufs=2))

        def tile(shape, dtype, name, tag=""):
            return sb.tile(shape, dtype, name=name, tag=tag or name, align_bytes=64)

        def quantize(values, width, name, tag=""):
            codes = tile([P, width], U32, name + "_codes", tag)
            scales = tile([P, width], U8, name + "_scales")
            nc.vector.quantize_mx(out=codes[:].bitcast(FP8X4), scales=scales[:], in_=values)
            return codes, scales

        tok_list = tile([P, I // 16], U16, "tok_list")
        note_list = tile([P, I // 16], U16, "note_list")
        col_list = tile([P, Q // 16], U16, "col_list")
        note_planes = [tile([P, U], F32, "note_plane%d" % j) for j in range(PACK)]
        q_raw = tile([P, PACK, Q], F32, "q_raw")
        q2_raw = tile([P, PACK, Q], F32, "q2_raw")
        key_pool = tile([P, T], I32, "key_pool")
        scale_pool = tile([P, T], U8, "scale_pool")
        factor = tile([P, PACK], F32, "factor")
        val_pool = [tile([P, T], F32, "val_pool%d" % b) for b in range(E_BLOCKS)]
        old_rows = [tile([P, M], F32, "old_rows%d" % b) for b in range(E_BLOCKS)]
        placed = [tile([P, M], F32, "placed%d" % b) for b in range(E_BLOCKS)]

        nc.gpsimd.memset(scale_pool[:].bitcast(I32), 0)
        scale_rows = keys_scales[0].bitcast(I32)
        notes_by_plane = notes.rearrange("(p j) u -> j p u", j=PACK)
        nc.sync.dma_start(out=note_planes[0][:], in_=notes_by_plane[0])
        nc.sync.dma_start(out=note_list[:], in_=offs2)
        nc.sync.dma_start(out=note_planes[1][:], in_=notes_by_plane[1])
        nc.sync.dma_start(out=tok_list[:], in_=offs)
        nc.sync.dma_start(out=note_planes[2][:], in_=notes_by_plane[2])
        for r in range(4):
            nc.sync.dma_start(out=scale_pool[r:P:32, :].bitcast(I32), in_=scale_rows[r:16:4, :])
        nc.sync.dma_start(out=note_planes[3][:], in_=notes_by_plane[3])
        nc.sync.dma_start(out=q2_raw[:], in_=query2.rearrange("(p j) q -> p j q", j=PACK))
        nc.sync.dma_start(out=q_raw[:], in_=query.rearrange("(p j) q -> p j q", j=PACK))
        nc.sync.dma_start(out=key_pool[:], in_=keys_words[0].rearrange("p t r -> p (t r)").bitcast(I32))
        nc.sync.dma_start(out=factor[:], in_=slot_factor.rearrange("o (p r) -> (o p) r", r=PACK))
        nc.sync.dma_start(out=col_list[:], in_=offs3)

        def load_vals(b):
            nc.sync.dma_start(out=val_pool[b][:], in_=vals[b * P : (b + 1) * P, :])

        def load_old(b):
            nc.sync.dma_start(out=old_rows[b][:], in_=old[b * P : (b + 1) * P, :])

        for b in range(E_BLOCKS):
            load_vals(b)
        for b in range(E_BLOCKS):
            load_old(b)

        ident = tile([P, P], F32, "ident")
        make_identity(nc, ident[:])
        for b in range(E_BLOCKS):
            engine = nc.gpsimd if b == E_BLOCKS - 1 else nc.vector
            engine.memset(placed[b][:], 0.0)

        key_scales = tile([P, I], U8, "key_scales")
        nc.vector.tensor_copy(out=key_scales[:], in_=scale_pool[:].indirect(tok_list[:]))

        note_picked = tile([P, PACK, I], BF16, "note_picked")
        for j in range(PACK):
            window = note_planes[j][:].indirect(note_list[:])
            if j % 2 == 0:
                nc.scalar.activation(out=note_picked[:, j, :], in_=window, func=ACT.Copy)
            else:
                nc.vector.tensor_copy(out=note_picked[:, j, :], in_=window)
        note_grouped = tile([P, I, PACK], BF16, "note_grouped")
        nc.vector.tensor_copy(
            out=note_grouped[:], in_=note_picked[:].rearrange("p j i -> p i j")
        )
        q2_grouped = tile([P, Q, PACK], BF16, "q2_grouped")
        q_grouped = tile([P, Q, PACK], BF16, "q_grouped")
        for grouped, raw in ((q2_grouped, q2_raw), (q_grouped, q_raw)):
            nc.scalar.copy(
                out=grouped[:], in_=raw[:].rearrange("p j q -> p q j")
            )
        note_codes, note_scales = quantize(note_grouped[:].rearrange("p i j -> p (i j)"), I, "note")
        q2_codes, q2_scales = quantize(q2_grouped[:].rearrange("p q j -> p (q j)"), Q, "q2")
        q_codes, q_scales = quantize(q_grouped[:].rearrange("p q j -> p (q j)"), Q, "q")
        key_codes = tile([P, I], U32, "key_codes")
        nc.vector.tensor_copy(out=key_codes[:], in_=key_pool[:].bitcast(U32).indirect(tok_list[:]))

        scores = [ps_one.tile([P, I], F32, name="scores%d" % h) for h in range(Q_BLOCKS)]
        for lhs_codes, lhs_scales, rhs_codes, rhs_scales, first in (
            (q2_codes, q2_scales, note_codes, note_scales, True),
            (q_codes, q_scales, key_codes, key_scales, False),
        ):
            for h in range(Q_BLOCKS):
                cols = slice(h * P, (h + 1) * P)
                nc.tensor.matmul_mx(
                    out=scores[h][:],
                    lhsT=lhs_codes[:, cols].bitcast(FP8X4),
                    lhsT_scale=lhs_scales[:, cols],
                    rhs=rhs_codes[:].bitcast(FP8X4),
                    rhs_scale=rhs_scales[:],
                    start=first,
                    stop=not first,
                )

        def pick_vals(b, on_vector, tag):
            picked = tile([P, I], BF16, "val_picked%d" % b, tag)
            window = val_pool[b][:].indirect(tok_list[:])
            if on_vector:
                nc.vector.tensor_copy(out=picked[:], in_=window)
            else:
                nc.scalar.activation(out=picked[:], in_=window, func=ACT.Copy)
            return picked

        def turn_vals(picked, pair_words):
            pairs = picked[:].bitcast(F32)
            turned = ps_two.tile([P, 2, P], F32, name="val_turned")
            for u in range(2):
                nc.tensor.transpose(turned[:, u, :], pairs[:, u::2], ident[:])
            nc.scalar.copy(out=pair_words.rearrange("p (e u) -> p e u", u=2), in_=turned[:].rearrange("p u e -> p e u"))

        def quantize_vals(b, pair_words, tag):
            return quantize(pair_words.bitcast(BF16), P, "val%d" % b, tag)

        sigs = []
        for h in range(Q_BLOCKS):
            sig = tile([P, PACK, P], F32, "sig%d" % h)
            nc.scalar.activation(out=sig[:], in_=scores[h][:].rearrange("q (s r) -> q r s", r=PACK), func=ACT.Sigmoid)
            sigs.append(sig)
        picked0 = pick_vals(0, True, "q_grouped")
        w_grouped = tile([P, Q, PACK], BF16, "w_grouped", "val_pool0")
        for h in range(Q_BLOCKS):
            sig_turned = ps_one.tile([P, PACK, P], F32, name="sig_turned%d" % h)
            for r in range(PACK):
                nc.tensor.transpose(sig_turned[:, r, :], sigs[h][:, r, :], ident[:])
            nc.vector.tensor_tensor(
                out=w_grouped[:, h * P : (h + 1) * P, :],
                in0=sig_turned[:].rearrange("s r q -> s q r"),
                in1=factor[:].unsqueeze(1).to_broadcast([P, P, PACK]),
                op=ALU.mult,
            )
        picked1 = pick_vals(1, False, "sig0")
        words0 = tile([P, 2 * P], F32, "words0", "val_pool1")
        turn_vals(picked0, words0[:])
        w_codes, w_scales = quantize(w_grouped[:].rearrange("s q r -> s (q r)"), Q, "w")
        val0 = quantize_vals(0, words0[:], "")

        def multiply(val_mx):
            val_codes, val_scales = val_mx
            acc = ps_two.tile([P, Q], F32, name="acc")
            nc.tensor.matmul_mx(
                out=acc[:],
                lhsT=val_codes[:].bitcast(FP8X4),
                lhsT_scale=val_scales[:],
                rhs=w_codes[:].bitcast(FP8X4),
                rhs_scale=w_scales[:],
                start=True,
                stop=True,
            )
            return acc

        def place_on_scalar(b, dense):
            nc.scalar.activation(out=placed[b][:].indirect(col_list[:]), in_=dense, func=ACT.Copy)

        def merge_larger(b, k):
            cols = slice(k * HALF, (k + 1) * HALF)
            larger = tile([P, HALF], F32, "larger%d_%d" % (b, k))
            nc.vector.tensor_tensor(out=larger[:], in0=placed[b][:, cols], in1=old_rows[b][:, cols], op=ALU.max)
            return larger

        def merge_store(b, k, larger, tag):
            cols = slice(k * HALF, (k + 1) * HALF)
            result = tile([P, HALF], F32, "result%d_%d" % (b, k), tag)
            nc.vector.scalar_tensor_tensor(
                out=result[:], in0=old_rows[b][:, cols], scalar=0.25, in1=larger[k][:], op0=ALU.mult, op1=ALU.add
            )
            nc.sync.dma_start(out=out[b * P : (b + 1) * P, cols], in_=result[:])
            return result

        def merge(b, tag=""):
            larger = [merge_larger(b, k) for k in range(2)]
            return [merge_store(b, k, larger, "") for k in range(2)]

        words1 = tile([P, 2 * P], F32, "words1")
        turn_vals(picked1, words1[:])
        picked2 = pick_vals(2, True, "val_pool1")
        dense0 = tile([P, Q], F32, "dense0")
        nc.scalar.copy(out=dense0[:], in_=multiply(val0)[:])
        place_on_scalar(0, dense0[:])
        val_mx = quantize_vals(1, words1[:], "val_pool2")
        picked3 = pick_vals(3, True, "words1")
        for b, picked in ((1, picked2), (2, picked3), (3, None)):
            dense = tile([P, Q], F32, "dense%d" % b)[:]
            nc.scalar.copy(out=dense, in_=multiply(val_mx)[:])
            if b < 3:
                words = tile([P, 2 * P], F32, "words%d" % (b + 1))[:]
                turn_vals(picked, words)
            if b == 1:
                val_mx = quantize_vals(b + 1, words, "val_pool3")
            place_on_scalar(b, dense)
            larger = [merge_larger(b - 1, 0)]
            if b == 2:
                val_mx = quantize_vals(b + 1, words, "larger0_1")
            larger.append(merge_larger(b - 1, 1))
            merge_store(b - 1, 0, larger, "")
            merge_store(b - 1, 1, larger, "")
        merge(3)
